import numpy as np
import ml_dtypes


def mxq(x, axis, fmt="e4m3"):
    dtype, down = {"e4m3": (ml_dtypes.float8_e4m3fn, 7), "e5m2": (ml_dtypes.float8_e5m2, 14)}[fmt]
    v = np.moveaxis(np.asarray(x, np.float32).astype(ml_dtypes.bfloat16).astype(np.float64), axis, -1)
    blocks = v.reshape(v.shape[:-1] + (-1, 32))
    amax = np.abs(blocks).max(-1, keepdims=True)
    byte = np.maximum(np.where(amax > 0, np.frexp(amax)[1] - 1 + 127, 0) - down, 1)
    scale = np.exp2(byte - 127.0)
    codes = (blocks / scale).astype(np.float32).astype(dtype).astype(np.float64)
    return np.moveaxis((codes * scale).reshape(v.shape), -1, axis)


WIDE = False


def mx_kscale(k):
    if not WIDE:
        return np.ones(k)
    levels = np.array([10, -10, 5, -5, 0])
    if k % 512:
        return np.exp2(np.random.permutation(np.resize(levels, k // 32))).repeat(32)
    a = np.empty((k // 512, 16))
    for p in range(k // 512):
        a[p, :8] = np.random.permutation(np.resize(levels, 8))
        for g in range(8):
            far = levels[np.abs(levels - a[p, g]) >= 10]
            a[p, g + 8] = far[np.random.randint(len(far))]
    return np.exp2(a.ravel()).repeat(32)


def f64(x):
    return np.asarray(x).astype(np.float64)


def striped(idx):
    return np.tile(np.asarray(idx).reshape(-1, 16).T, (8, 1)).astype(np.uint16)


def unstriped(offs):
    return offs[:16].T.reshape(-1).astype(np.int64)


def striped8(idx):
    return np.asarray(idx).reshape(8, -1, 16).transpose(0, 2, 1).reshape(128, -1).astype(np.uint16)


def unstriped8(offs):
    return offs.reshape(8, 16, -1).transpose(0, 2, 1).reshape(8, -1).astype(np.int64)


def pick8(x, idx, run):
    r = np.arange(len(x))
    return x[r[:, None], idx[r % (8 * run) // run]]


E2M1 = np.array([0.0, 0.5, 1.0, 1.5, 2.0, 3.0, 4.0, 6.0, -0.0, -0.5, -1.0, -1.5, -2.0, -3.0, -4.0, -6.0])


def pack_weight(w, fmt):
    k, n = w.shape
    w = f64(np.asarray(w, np.float32).astype(ml_dtypes.bfloat16)).reshape(k // 32, 32, n)
    amax = np.abs(w).max(1)
    if fmt == "e4m3":
        byte = np.frexp(amax)[1] - 1 + 127 - 7
    else:
        mant, ex = np.frexp(amax / 6.0)
        byte = np.where(mant > 0.5, ex, ex - 1) + 127
    byte = np.clip(np.where(amax > 0, byte, 1), 1, 254)
    scaled = (w * np.exp2(127.0 - byte)[:, None, :]).reshape(k, n).astype(np.float32)
    by_word = np.ascontiguousarray(scaled.reshape(k // 512, 128, 4, n).transpose(0, 1, 3, 2))
    if fmt == "e4m3":
        words = by_word.astype(ml_dtypes.float8_e4m3fn).view(np.uint8)
    else:
        c = by_word.astype(ml_dtypes.float4_e2m1fn).view(np.uint8) & 0xF
        words = (c[..., 0::2] | (c[..., 1::2] << 4)).reshape(k // 512, 128, 2 * n)
    return np.ascontiguousarray(words), np.ascontiguousarray(byte.astype(np.uint8).reshape(k // 512, 16, n))


def unpack_weight(words, scales, fmt):
    g, _, n = scales.shape
    words = np.ascontiguousarray(words).reshape(g, 128, n, -1)
    if fmt == "e4m3":
        vals = words.view(ml_dtypes.float8_e4m3fn).astype(np.float64)
    else:
        nib = np.empty((g, 128, n, 4), np.uint8)
        nib[..., 0::2] = words & 0xF
        nib[..., 1::2] = words >> 4
        vals = E2M1[nib]
    vals = vals * np.repeat(np.exp2(scales.astype(np.float64) - 127.0), 8, axis=1)[..., None]
    return vals.transpose(0, 1, 3, 2).reshape(g * 512, n)


K, J, R, T, F, G, O, C, S, N = 512, 512, 512, 1024, 1024, 1024, 256, 512, 256, 256


def setup_inputs():
    n = np.random.standard_normal
    idx = np.random.permutation(T)[:J]
    idx2 = np.stack([np.random.permutation(F)[:R] for _ in range(8)])
    idx3 = np.stack([np.random.permutation(G)[:R] for _ in range(8)])
    idx4 = np.stack([np.random.permutation(J)[:S] for _ in range(8)])
    idx5 = np.stack([np.random.permutation(C)[:S] for _ in range(8)])
    idx6 = np.stack([np.random.permutation(C)[:O] for _ in range(8)])
    idx7 = np.random.permutation(T)[:O]
    fk = mx_kscale(K)
    fr = mx_kscale(R)
    xtp = pack_weight(n((K, T)) * fk[:, None], "e4m3")
    wbp = pack_weight(n((R, N)) * 1 / np.sqrt(R) / fr[:, None], "e4m3")
    wsp = pack_weight(n((K, N)) * 1 / np.sqrt(K) / fk[:, None], "e2m1")
    return {
        "xt_words": xtp[0],
        "xt_scales": xtp[1],
        "ua": (np.random.randint(-7, 8, (K, F)).astype(np.float64)).astype(np.float32),
        "ub": (np.random.randint(-7, 8, (K, G)).astype(np.float64)).astype(np.float32),
        "ha": ((np.random.randint(10, 25, (K, 1)) / 1024.0) / fk[:, None]).astype(np.float32),
        "hb": ((np.random.randint(4, 13, (K, 1)) / 1024.0) / fk[:, None]).astype(np.float32),
        "sa": (np.random.uniform(0.5, 1.6, (R, 1)) * fr[:, None]).astype(np.float32),
        "sb": (np.random.uniform(0.5, 1.6, (R, 1))).astype(np.float32),
        "wb_words": wbp[0],
        "wb_scales": wbp[1],
        "ws_words": wsp[0],
        "ws_scales": wsp[1],
        "offs": striped(idx),
        "offs2": striped8(idx2),
        "offs3": striped8(idx3),
        "offs4": striped8(idx4),
        "offs5": striped8(idx5),
        "offs6": striped8(idx6),
        "offs7": striped(idx7),
    }


def reference(xt_words, xt_scales, ua, ub, ha, hb, sa, sb, wb_words, wb_scales, ws_words, ws_scales, offs, offs2, offs3, offs4, offs5, offs6, offs7):
    idx = unstriped(offs)
    idx2 = unstriped8(offs2)
    idx3 = unstriped8(offs3)
    idx4 = unstriped8(offs4)
    idx5 = unstriped8(offs5)
    idx6 = unstriped8(offs6)
    idx7 = unstriped(offs7)
    xtu = unpack_weight(xt_words, xt_scales, "e4m3")
    wbu = unpack_weight(wb_words, wb_scales, "e4m3")
    wsu = unpack_weight(ws_words, ws_scales, "e2m1")
    wc = pick8(f64(ua), idx2, 64) * f64(ha) + pick8(f64(ub), idx3, 64) * f64(hb)
    wcq = mxq(wc, 0, "e4m3")
    xtidxg = xtu[:, idx]
    a = wcq.T @ xtidxg
    h1 = pick8(a, idx4, 64) * f64(sa)
    pw = np.zeros((R, C))
    pw[np.arange(R)[:, None], idx5[np.arange(R) % 512 // 64]] = h1
    g1 = np.maximum(pw, 0.0)
    hid = pick8(g1, idx6, 64) * f64(sb)
    hidq = mxq(hid, 0, "e4m3")
    xtidx7g = xtu[:, idx7]
    y = wbu.T @ hidq + wsu.T @ xtidx7g
    return y

@@ -1,0 +1,231 @@
+from contextlib import ExitStack
+
+import concourse.mybir as mybir
+
+K, J, R, T, F, G, O, C, S, N = 512, 512, 512, 1024, 1024, 1024, 256, 512, 256, 256
+FLOPS = 2 * K * R * J + 2 * R * N * O + 2 * K * N * O
+
+F32 = mybir.dt.float32
+BF16 = mybir.dt.bfloat16
+I32 = mybir.dt.int32
+U32 = mybir.dt.uint32
+U16 = mybir.dt.uint16
+U8 = mybir.dt.uint8
+FP8X4 = mybir.dt.float8_e4m3fn_x4
+FP4X4 = mybir.dt.float4_e2m1fn_x4
+ACT = mybir.ActivationFunctionType
+ALU = mybir.AluOpType
+
+P = 128
+PACK = 4
+LIST_ROWS = 16
+
+
+def tile_picked_tokens_twobooks_one_weighedposting_further_plain_kernel(
+    tc, xt_words, xt_scales, ua, ub, ha, hb, sa, sb, wb_words, wb_scales, ws_words, ws_scales,
+    offs, offs2, offs3, offs4, offs5, offs6, offs7, out,
+):
+    nc = tc.nc
+    with ExitStack() as ctx:
+        keep = ctx.enter_context(tc.tile_pool(name="keep", bufs=1))
+        ring = ctx.enter_context(tc.tile_pool(name="ring", bufs=2))
+        psum = ctx.enter_context(tc.psum_pool(name="psum", bufs=1))
+
+        def load_list(dram, name):
+            tile = keep.tile(list(dram.shape), U16, name=name)
+            nc.sync.dma_start(tile[:], dram)
+            return tile
+
+        def load_column(dram, name):
+            tile = keep.tile([P, PACK], F32, name=name)
+            nc.sync.dma_start(tile[:], dram.rearrange("(p t) o -> p (t o)", t=PACK))
+            return tile
+
+        def load_rows(dram, t, name):
+            tile = keep.tile([P, dram.shape[1]], F32, name=name)
+            nc.sync.dma_start(tile[:], dram.rearrange("(p t) f -> p t f", t=PACK)[:, t, :])
+            return tile
+
+        def cleared_scales(width, name):
+            tile = keep.tile([P, width], U8, name=name, align_bytes=64)
+            nc.vector.memset(tile[:].bitcast(I32), 0)
+            return tile
+
+        def load_scales(queue, tile, dram):
+            for q in range(4):
+                queue.dma_start(
+                    tile[32 * q : 32 * q + 4, :].bitcast(I32), dram[0, 4 * q : 4 * q + 4, :].bitcast(I32)
+                )
+
+        def load_words(dram, width, name):
+            tile = keep.tile([P, width], U32, name=name, align_bytes=64)
+            nc.sync.dma_start(tile[:].bitcast(I32), dram[0].rearrange("p n t -> p (n t)").bitcast(I32))
+            return tile
+
+        xs_win = cleared_scales(T, "xs_win")
+        ws_sc = cleared_scales(N, "ws_sc")
+        wb_sc = cleared_scales(N, "wb_sc")
+        board = [keep.tile([P, C], F32, name="board%d" % t) for t in range(PACK)]
+        for t in range(PACK):
+            nc.vector.memset(board[t][:], 0.0)
+
+        ua_rows, ub_rows = [], []
+        ua_rows.append(load_rows(ua, 0, "ua0"))
+        l2 = load_list(offs2, "l2")
+        ha4 = load_column(ha, "ha4")
+        ub_rows.append(load_rows(ub, 0, "ub0"))
+        l3 = load_list(offs3, "l3")
+        hb4 = load_column(hb, "hb4")
+        ua_rows.append(load_rows(ua, 1, "ua1"))
+        ub_rows.append(load_rows(ub, 1, "ub1"))
+        ua_rows.append(load_rows(ua, 2, "ua2"))
+        xs_stage = keep.tile([P, 2, T], U8, name="xs_stage")
+        for half in range(2):
+            nc.sync.dma_start(
+                xs_stage[64 * half : 64 * half + 4].bitcast(I32),
+                xt_scales[0, 8 * half : 8 * half + 8, :].rearrange("(q i) w -> i q w", i=4).bitcast(I32),
+            )
+        l1 = load_list(offs, "l1")
+        xt_win = load_words(xt_words, T, "xt_win")
+        l7 = load_list(offs7, "l7")
+        ub_rows.append(load_rows(ub, 2, "ub2"))
+        ua_rows.append(load_rows(ua, 3, "ua3"))
+        ub_rows.append(load_rows(ub, 3, "ub3"))
+        for q in range(4):
+            nc.vector.tensor_copy(
+                xs_win[32 * q : 32 * q + 4, :].bitcast(I32),
+                xs_stage[64 * (q // 2) : 64 * (q // 2) + 4, q % 2, :].bitcast(I32),
+            )
+        l4 = load_list(offs4, "l4")
+        sa4 = load_column(sa, "sa4")
+        l5 = load_list(offs5, "l5")
+        ws_w = keep.tile([P, 2 * N], U8, name="ws_w", align_bytes=64)
+        nc.sync.dma_start(ws_w[:].bitcast(I32), ws_words[0].bitcast(I32))
+        load_scales(nc.sync, ws_sc, ws_scales)
+        l6 = load_list(offs6, "l6")
+        sb4 = load_column(sb, "sb4")
+        wb_w = load_words(wb_words, N, "wb_w")
+        load_scales(nc.sync, wb_sc, wb_scales)
+
+        def part(lst, lo, hi):
+            return lst[:, lo // LIST_ROWS : hi // LIST_ROWS]
+
+        xj_sc = keep.tile([P, J], U8, name="xj_sc", align_bytes=64)
+        xo_sc = keep.tile([P, O], U8, name="xo_sc", align_bytes=64)
+        xj_w = keep.tile([P, J], U32, name="xj_w", align_bytes=64)
+        xo_w = keep.tile([P, O], U32, name="xo_w", align_bytes=64)
+        nc.vector.tensor_copy(xj_sc[:], xs_win[:].indirect(l1[:]))
+        nc.vector.tensor_copy(xo_sc[:], xs_win[:].indirect(l7[:]))
+        nc.vector.tensor_copy(xj_w[:], xt_win[:].indirect(l1[:]))
+        nc.vector.tensor_copy(xo_w[:], xt_win[:].indirect(l7[:]))
+
+        wc = keep.tile([P, PACK, R], BF16, name="wc")
+        for t in range(PACK):
+            ga = keep.tile([P, R], F32, name="ga%d" % t)
+            gb = keep.tile([P, R], F32, name="gb%d" % t)
+            nc.scalar.activation(ga[:], ua_rows[t][:].indirect(l2[:]), ACT.Copy, scale=ha4[:, t : t + 1])
+            pieces = [(0, R)] if t < PACK - 1 else [(0, R // 2), (R // 2, R)]
+            for lo, hi in pieces:
+                nc.scalar.activation(
+                    gb[:, lo:hi], ub_rows[t][:].indirect(part(l3, lo, hi)), ACT.Copy, scale=hb4[:, t : t + 1]
+                )
+                nc.vector.tensor_tensor(wc[:, t, lo:hi], ga[:, lo:hi], gb[:, lo:hi], ALU.add)
+
+        wc_dealt = wc[:].rearrange("p t (m u) -> p u m t", u=PACK)
+
+        def weave(u):
+            woven = ring.tile([P, P, PACK], BF16, name="woven", align_bytes=64)
+            nc.vector.tensor_copy(woven[:], wc_dealt[:, u])
+            return woven
+
+        a_parts = []
+        woven = {0: weave(0), 1: weave(1)}
+        for u in range(PACK):
+            wq_w = keep.tile([P, P], U32, name="wq_w%d" % u, align_bytes=64)
+            wq_sc = keep.tile([P, P], U8, name="wq_sc%d" % u, align_bytes=64)
+            nc.vector.quantize_mx(
+                out=wq_w[:].bitcast(FP8X4), scales=wq_sc[:], in_=woven[u][:].rearrange("p m t -> p (m t)")
+            )
+            parts = []
+            for lo, hi in [(0, J // 2), (J // 2, J)] if u == 0 else [(0, J)]:
+                a_ps = psum.tile([P, hi - lo], F32, name="a_ps", bufs=4)
+                nc.tensor.matmul_mx(
+                    out=a_ps[:], lhsT=wq_w[:].bitcast(FP8X4), lhsT_scale=wq_sc[:],
+                    rhs=xj_w[:, lo:hi].bitcast(FP8X4), rhs_scale=xj_sc[:, lo:hi], start=True, stop=True,
+                )
+                parts.append((lo, hi, a_ps))
+            a_parts.append(parts)
+            if u + 2 < PACK:
+                woven[u + 2] = weave(u + 2)
+            if u == 0:
+                a_first = keep.tile([P, J], F32, name="a_sb0")
+                for lo, hi, a_ps in parts:
+                    nc.scalar.copy(a_first[:, lo:hi], a_ps[:])
+
+        H = O // 2
+        y_ps = {}
+        for h in range(2):
+            for nt in range(N // P):
+                y_ps[h, nt] = psum.tile([P, H], F32, name="y_ps%d%d" % (h, nt))
+                nc.tensor.matmul_mx(
+                    out=y_ps[h, nt][:],
+                    lhsT=ws_w[:, 2 * P * nt : 2 * P * (nt + 1)].bitcast(FP4X4),
+                    lhsT_scale=ws_sc[:, P * nt : P * (nt + 1)],
+                    rhs=xo_w[:, H * h : H * (h + 1)].bitcast(FP8X4),
+                    rhs_scale=xo_sc[:, H * h : H * (h + 1)],
+                    start=True, stop=False,
+                )
+
+        for u in range(PACK):
+            if u == 0:
+                a_sb = a_first
+            else:
+                a_sb = keep.tile([P, J], F32, name="a_sb%d" % u, tag="a_sb%d" % u)
+                a_ps = a_parts[u][0][2]
+                if u == 1:
+                    nc.vector.tensor_copy(a_sb[:], a_ps[:])
+                else:
+                    nc.scalar.copy(a_sb[:], a_ps[:])
+            h1 = keep.tile([P, S], F32, name="h1_%d" % u, tag="h1_%d" % u)
+            nc.scalar.activation(h1[:], a_sb[:].indirect(l4[:]), ACT.Copy, scale=sa4[:, u : u + 1])
+            if u == 0:
+                pos = h1
+            else:
+                pos = keep.tile([P, S], F32, name="pos%d" % u)
+                nc.scalar.activation(pos[:], h1[:], ACT.Relu)
+            nc.vector.tensor_copy(board[u][:].indirect(l5[:]), pos[:])
+
+        g1_first = keep.tile([P, C], F32, name="g1_first", tag="a_sb3")
+        nc.scalar.activation(g1_first[:], board[0][:], ACT.Relu)
+        g1 = [g1_first] + board[1:]
+
+        hid = keep.tile([P, PACK, O], BF16, name="hid", tag="h1_3")
+        for u in range(PACK):
+            pieces = [(0, O)] if u < PACK - 1 else [(0, H), (H, O)]
+            for lo, hi in pieces:
+                nc.scalar.activation(
+                    hid[:, u, lo:hi], g1[u][:].indirect(part(l6, lo, hi)), ACT.Copy, scale=sb4[:, u : u + 1]
+                )
+
+        for h in range(2):
+            hw = keep.tile([P, H, PACK], BF16, name="hw%d" % h, align_bytes=64)
+            nc.vector.tensor_copy(hw[:], hid[:, :, H * h : H * (h + 1)].rearrange("p t o -> p o t"))
+            hq_w = keep.tile([P, H], U32, name="hq_w%d" % h, align_bytes=64)
+            hq_sc = keep.tile([P, H], U8, name="hq_sc%d" % h, align_bytes=64)
+            nc.vector.quantize_mx(
+                out=hq_w[:].bitcast(FP8X4), scales=hq_sc[:], in_=hw[:].rearrange("p o t -> p (o t)")
+            )
+            res = keep.tile([P, N // P, H], F32, name="res%d" % h)
+            for nt in range(N // P):
+                nc.tensor.matmul_mx(
+                    out=y_ps[h, nt][:],
+                    lhsT=wb_w[:, P * nt : P * (nt + 1)].bitcast(FP8X4),
+                    lhsT_scale=wb_sc[:, P * nt : P * (nt + 1)],
+                    rhs=hq_w[:].bitcast(FP8X4), rhs_scale=hq_sc[:],
+                    start=False, stop=True,
+                )
+                if nt == 0:
+                    nc.scalar.copy(res[:, nt, :], y_ps[h, nt][:])
+                else:
+                    nc.vector.tensor_copy(res[:, nt, :], y_ps[h, nt][:])
+            nc.sync.dma_start(out[:, H * h : H * (h + 1)].rearrange("(n p) o -> p n o", p=P), res[:])

@@ -62,6 +62,10 @@ def tile_picked_tokens_twobooks_one_weighedposting_further_plain_kernel(
             nc.sync.dma_start(tile[:].bitcast(I32), dram[0].rearrange("p n t -> p (n t)").bitcast(I32))
             return tile
 
+        warm_in = keep.tile([P, 1], F32, name="warm_in")
+        warm_out = keep.tile([P, 1], F32, name="warm_out")
+        nc.vector.memset(warm_in[:], 0.0)
+        nc.scalar.activation(warm_out[:], warm_in[:], ACT.Copy)
         xs_win = cleared_scales(T, "xs_win")
         ws_sc = cleared_scales(N, "ws_sc")
         wb_sc = cleared_scales(N, "wb_sc")

@@ -36,9 +36,9 @@ def tile_picked_tokens_twobooks_one_weighedposting_further_plain_kernel(
             nc.sync.dma_start(tile[:], dram)
             return tile
 
-        def load_column(dram, name):
+        def load_column(queue, dram, name):
             tile = keep.tile([P, PACK], F32, name=name)
-            nc.sync.dma_start(tile[:], dram.rearrange("(p t) o -> p (t o)", t=PACK))
+            queue.dma_start(tile[:], dram.rearrange("(p t) o -> p (t o)", t=PACK))
             return tile
 
         def load_rows(dram, t, name):
@@ -69,31 +69,31 @@ def tile_picked_tokens_twobooks_one_weighedposting_further_plain_kernel(
         xs_win = cleared_scales(T, "xs_win")
         ws_sc = cleared_scales(N, "ws_sc")
         wb_sc = cleared_scales(N, "wb_sc")
-        board = [keep.tile([P, C], F32, name="board%d" % t) for t in range(PACK)]
-        for t in range(PACK):
-            nc.vector.memset(board[t][:], 0.0)
-
-        ua_rows, ub_rows = [], []
-        ua_rows.append(load_rows(ua, 0, "ua0"))
-        l2 = load_list(offs2, "l2")
-        ha4 = load_column(ha, "ha4")
-        ub_rows.append(load_rows(ub, 0, "ub0"))
-        l3 = load_list(offs3, "l3")
-        hb4 = load_column(hb, "hb4")
-        ua_rows.append(load_rows(ua, 1, "ua1"))
-        ub_rows.append(load_rows(ub, 1, "ub1"))
-        ua_rows.append(load_rows(ua, 2, "ua2"))
         xs_stage = keep.tile([P, 2, T], U8, name="xs_stage")
         for half in range(2):
             nc.sync.dma_start(
                 xs_stage[64 * half : 64 * half + 4].bitcast(I32),
                 xt_scales[0, 8 * half : 8 * half + 8, :].rearrange("(q i) w -> i q w", i=4).bitcast(I32),
             )
+        board = [keep.tile([P, C], F32, name="board%d" % t) for t in range(PACK)]
+        for t in range(PACK):
+            nc.gpsimd.memset(board[t][:], 0.0)
+
+        ua_rows, ub_rows = [], []
+        ua_rows.append(load_rows(ua, 0, "ua0"))
+        l2 = load_list(offs2, "l2")
+        ha4 = load_column(nc.sync, ha, "ha4")
         l1 = load_list(offs, "l1")
-        xt_win = load_words(xt_words, T, "xt_win")
+        ub_rows.append(load_rows(ub, 0, "ub0"))
+        l3 = load_list(offs3, "l3")
+        hb4 = load_column(nc.sync, hb, "hb4")
+        ua_rows.append(load_rows(ua, 1, "ua1"))
+        ub_rows.append(load_rows(ub, 1, "ub1"))
         l7 = load_list(offs7, "l7")
+        ua_rows.append(load_rows(ua, 2, "ua2"))
         ub_rows.append(load_rows(ub, 2, "ub2"))
         ua_rows.append(load_rows(ua, 3, "ua3"))
+        xt_win = load_words(xt_words, T, "xt_win")
         ub_rows.append(load_rows(ub, 3, "ub3"))
         for q in range(4):
             nc.vector.tensor_copy(
@@ -101,13 +101,13 @@ def tile_picked_tokens_twobooks_one_weighedposting_further_plain_kernel(
                 xs_stage[64 * (q // 2) : 64 * (q // 2) + 4, q % 2, :].bitcast(I32),
             )
         l4 = load_list(offs4, "l4")
-        sa4 = load_column(sa, "sa4")
+        sa4 = load_column(nc.sync, sa, "sa4")
         l5 = load_list(offs5, "l5")
         ws_w = keep.tile([P, 2 * N], U8, name="ws_w", align_bytes=64)
         nc.sync.dma_start(ws_w[:].bitcast(I32), ws_words[0].bitcast(I32))
         load_scales(nc.sync, ws_sc, ws_scales)
         l6 = load_list(offs6, "l6")
-        sb4 = load_column(sb, "sb4")
+        sb4 = load_column(nc.sync, sb, "sb4")
         wb_w = load_words(wb_words, N, "wb_w")
         load_scales(nc.sync, wb_sc, wb_scales)
 
@@ -117,33 +117,35 @@ def tile_picked_tokens_twobooks_one_weighedposting_further_plain_kernel(
         xj_sc = keep.tile([P, J], U8, name="xj_sc", align_bytes=64)
         xo_sc = keep.tile([P, O], U8, name="xo_sc", align_bytes=64)
         xj_w = keep.tile([P, J], U32, name="xj_w", align_bytes=64)
-        xo_w = keep.tile([P, O], U32, name="xo_w", align_bytes=64)
         nc.vector.tensor_copy(xj_sc[:], xs_win[:].indirect(l1[:]))
         nc.vector.tensor_copy(xo_sc[:], xs_win[:].indirect(l7[:]))
         nc.vector.tensor_copy(xj_w[:], xt_win[:].indirect(l1[:]))
-        nc.vector.tensor_copy(xo_w[:], xt_win[:].indirect(l7[:]))
 
-        wc = keep.tile([P, PACK, R], BF16, name="wc")
+        LAST = PACK - 1
+        EARLY = 2
+        wc_late = keep.tile([P, PACK, P, 2], BF16, name="wc_late")
+        woven = {u: ring.tile([P, P, PACK], BF16, name="woven", align_bytes=64) for u in range(EARLY)}
         for t in range(PACK):
             ga = keep.tile([P, R], F32, name="ga%d" % t)
             gb = keep.tile([P, R], F32, name="gb%d" % t)
+            ga4 = ga[:].rearrange("p (m u) -> p m u", u=PACK)
+            gb4 = gb[:].rearrange("p (m u) -> p m u", u=PACK)
             nc.scalar.activation(ga[:], ua_rows[t][:].indirect(l2[:]), ACT.Copy, scale=ha4[:, t : t + 1])
-            pieces = [(0, R)] if t < PACK - 1 else [(0, R // 2), (R // 2, R)]
-            for lo, hi in pieces:
+            for lo, hi in [(0, R)] if t < LAST else [(0, R // 2), (R // 2, R)]:
                 nc.scalar.activation(
                     gb[:, lo:hi], ub_rows[t][:].indirect(part(l3, lo, hi)), ACT.Copy, scale=hb4[:, t : t + 1]
                 )
-                nc.vector.tensor_tensor(wc[:, t, lo:hi], ga[:, lo:hi], gb[:, lo:hi], ALU.add)
-
-        wc_dealt = wc[:].rearrange("p t (m u) -> p u m t", u=PACK)
+                ms = slice(lo // PACK, hi // PACK)
+                for u in range(EARLY):
+                    nc.vector.tensor_tensor(woven[u][:, ms, t], ga4[:, ms, u], gb4[:, ms, u], ALU.add)
+                nc.vector.tensor_tensor(wc_late[:, t, ms], ga4[:, ms, EARLY:], gb4[:, ms, EARLY:], ALU.add)
 
         def weave(u):
-            woven = ring.tile([P, P, PACK], BF16, name="woven", align_bytes=64)
-            nc.vector.tensor_copy(woven[:], wc_dealt[:, u])
-            return woven
+            full = ring.tile([P, P, PACK], BF16, name="woven", align_bytes=64)
+            nc.vector.tensor_copy(full[:], wc_late[:, :, :, u - EARLY].rearrange("p t m -> p m t"))
+            return full
 
         a_parts = []
-        woven = {0: weave(0), 1: weave(1)}
         for u in range(PACK):
             wq_w = keep.tile([P, P], U32, name="wq_w%d" % u, align_bytes=64)
             wq_sc = keep.tile([P, P], U8, name="wq_sc%d" % u, align_bytes=64)
@@ -167,6 +169,27 @@ def tile_picked_tokens_twobooks_one_weighedposting_further_plain_kernel(
                     nc.scalar.copy(a_first[:, lo:hi], a_ps[:])
 
         H = O // 2
+        for u in range(PACK):
+            if u == 0:
+                a_sb = a_first
+            else:
+                a_sb = keep.tile([P, J], F32, name="a_sb%d" % u, tag="a_sb%d" % u)
+                a_ps = a_parts[u][0][2]
+                if u == 1:
+                    nc.vector.tensor_copy(a_sb[:], a_ps[:])
+                else:
+                    nc.scalar.copy(a_sb[:], a_ps[:])
+            h1 = keep.tile([P, S], F32, name="h1_%d" % u, tag="a_sb3" if u == 1 else "h1_%d" % u)
+            nc.scalar.activation(h1[:], a_sb[:].indirect(l4[:]), ACT.Copy, scale=sa4[:, u : u + 1])
+            if u == 0:
+                pos = h1
+            else:
+                pos = keep.tile([P, S], F32, name="pos%d" % u, tag="pos%d" % u, align_bytes=64)
+                nc.scalar.activation(pos[:], h1[:], ACT.Relu)
+            nc.vector.tensor_copy(board[u][:].indirect(l5[:]), pos[:])
+
+        xo_w = keep.tile([P, O], U32, name="xo_w", tag="pos3", align_bytes=64)
+        nc.vector.tensor_copy(xo_w[:], xt_win[:].indirect(l7[:]))
         y_ps = {}
         for h in range(2):
             for nt in range(N // P):
@@ -179,25 +202,6 @@ def tile_picked_tokens_twobooks_one_weighedposting_further_plain_kernel(
                     rhs_scale=xo_sc[:, H * h : H * (h + 1)],
                     start=True, stop=False,
                 )
-
-        for u in range(PACK):
-            if u == 0:
-                a_sb = a_first
-            else:
-                a_sb = keep.tile([P, J], F32, name="a_sb%d" % u, tag="a_sb%d" % u)
-                a_ps = a_parts[u][0][2]
-                if u == 1:
-                    nc.vector.tensor_copy(a_sb[:], a_ps[:])
-                else:
-                    nc.scalar.copy(a_sb[:], a_ps[:])
-            h1 = keep.tile([P, S], F32, name="h1_%d" % u, tag="h1_%d" % u)
-            nc.scalar.activation(h1[:], a_sb[:].indirect(l4[:]), ACT.Copy, scale=sa4[:, u : u + 1])
-            if u == 0:
-                pos = h1
-            else:
-                pos = keep.tile([P, S], F32, name="pos%d" % u)
-                nc.scalar.activation(pos[:], h1[:], ACT.Relu)
-            nc.vector.tensor_copy(board[u][:].indirect(l5[:]), pos[:])
 
         g1_first = keep.tile([P, C], F32, name="g1_first", tag="a_sb3")
         nc.scalar.activation(g1_first[:], board[0][:], ACT.Relu)

from contextlib import ExitStack

import concourse.mybir as mybir

K, J, R, T, F, G, O, C, S, N = 512, 512, 512, 1024, 1024, 1024, 256, 512, 256, 256
FLOPS = 2 * K * R * J + 2 * R * N * O + 2 * K * N * O

F32 = mybir.dt.float32
BF16 = mybir.dt.bfloat16
I32 = mybir.dt.int32
U32 = mybir.dt.uint32
U16 = mybir.dt.uint16
U8 = mybir.dt.uint8
FP8X4 = mybir.dt.float8_e4m3fn_x4
FP4X4 = mybir.dt.float4_e2m1fn_x4
ACT = mybir.ActivationFunctionType
ALU = mybir.AluOpType

P = 128
PACK = 4
LIST_ROWS = 16


def tile_picked_tokens_twobooks_one_weighedposting_further_plain_kernel(
    tc, xt_words, xt_scales, ua, ub, ha, hb, sa, sb, wb_words, wb_scales, ws_words, ws_scales,
    offs, offs2, offs3, offs4, offs5, offs6, offs7, out,
):
    nc = tc.nc
    with ExitStack() as ctx:
        keep = ctx.enter_context(tc.tile_pool(name="keep", bufs=1))
        ring = ctx.enter_context(tc.tile_pool(name="ring", bufs=2))
        psum = ctx.enter_context(tc.psum_pool(name="psum", bufs=1))

        def load_list(dram, name):
            tile = keep.tile(list(dram.shape), U16, name=name)
            nc.sync.dma_start(tile[:], dram)
            return tile

        def load_column(queue, dram, name):
            tile = keep.tile([P, PACK], F32, name=name)
            queue.dma_start(tile[:], dram.rearrange("(p t) o -> p (t o)", t=PACK))
            return tile

        def load_rows(dram, t, name):
            tile = keep.tile([P, dram.shape[1]], F32, name=name)
            nc.sync.dma_start(tile[:], dram.rearrange("(p t) f -> p t f", t=PACK)[:, t, :])
            return tile

        def cleared_scales(width, name):
            tile = keep.tile([P, width], U8, name=name, align_bytes=64)
            nc.vector.memset(tile[:].bitcast(I32), 0)
            return tile

        def load_scales(queue, tile, dram):
            for q in range(4):
                queue.dma_start(
                    tile[32 * q : 32 * q + 4, :].bitcast(I32), dram[0, 4 * q : 4 * q + 4, :].bitcast(I32)
                )

        def load_words(dram, width, name):
            tile = keep.tile([P, width], U32, name=name, align_bytes=64)
            nc.sync.dma_start(tile[:].bitcast(I32), dram[0].rearrange("p n t -> p (n t)").bitcast(I32))
            return tile

        warm_in = keep.tile([P, 1], F32, name="warm_in")
        warm_out = keep.tile([P, 1], F32, name="warm_out")
        nc.vector.memset(warm_in[:], 0.0)
        nc.scalar.activation(warm_out[:], warm_in[:], ACT.Copy)
        xs_win = cleared_scales(T, "xs_win")
        ws_sc = cleared_scales(N, "ws_sc")
        wb_sc = cleared_scales(N, "wb_sc")
        xs_stage = keep.tile([P, 2, T], U8, name="xs_stage")
        for half in range(2):
            nc.sync.dma_start(
                xs_stage[64 * half : 64 * half + 4].bitcast(I32),
                xt_scales[0, 8 * half : 8 * half + 8, :].rearrange("(q i) w -> i q w", i=4).bitcast(I32),
            )
        board = [keep.tile([P, C], F32, name="board%d" % t) for t in range(PACK)]
        for t in range(PACK):
            nc.gpsimd.memset(board[t][:], 0.0)

        ua_rows, ub_rows = [], []
        ua_rows.append(load_rows(ua, 0, "ua0"))
        l2 = load_list(offs2, "l2")
        ha4 = load_column(nc.sync, ha, "ha4")
        l1 = load_list(offs, "l1")
        ub_rows.append(load_rows(ub, 0, "ub0"))
        l3 = load_list(offs3, "l3")
        hb4 = load_column(nc.sync, hb, "hb4")
        ua_rows.append(load_rows(ua, 1, "ua1"))
        ub_rows.append(load_rows(ub, 1, "ub1"))
        l7 = load_list(offs7, "l7")
        ua_rows.append(load_rows(ua, 2, "ua2"))
        ub_rows.append(load_rows(ub, 2, "ub2"))
        ua_rows.append(load_rows(ua, 3, "ua3"))
        xt_win = load_words(xt_words, T, "xt_win")
        ub_rows.append(load_rows(ub, 3, "ub3"))
        for q in range(4):
            nc.vector.tensor_copy(
                xs_win[32 * q : 32 * q + 4, :].bitcast(I32),
                xs_stage[64 * (q // 2) : 64 * (q // 2) + 4, q % 2, :].bitcast(I32),
            )
        l4 = load_list(offs4, "l4")
        sa4 = load_column(nc.sync, sa, "sa4")
        l5 = load_list(offs5, "l5")
        ws_w = keep.tile([P, 2 * N], U8, name="ws_w", align_bytes=64)
        nc.sync.dma_start(ws_w[:].bitcast(I32), ws_words[0].bitcast(I32))
        load_scales(nc.sync, ws_sc, ws_scales)
        l6 = load_list(offs6, "l6")
        sb4 = load_column(nc.sync, sb, "sb4")
        wb_w = load_words(wb_words, N, "wb_w")
        load_scales(nc.sync, wb_sc, wb_scales)

        def part(lst, lo, hi):
            return lst[:, lo // LIST_ROWS : hi // LIST_ROWS]

        xj_sc = keep.tile([P, J], U8, name="xj_sc", align_bytes=64)
        xo_sc = keep.tile([P, O], U8, name="xo_sc", align_bytes=64)
        xj_w = keep.tile([P, J], U32, name="xj_w", align_bytes=64)
        nc.vector.tensor_copy(xj_sc[:], xs_win[:].indirect(l1[:]))
        nc.vector.tensor_copy(xo_sc[:], xs_win[:].indirect(l7[:]))
        nc.vector.tensor_copy(xj_w[:], xt_win[:].indirect(l1[:]))

        LAST = PACK - 1
        EARLY = 2
        wc_late = keep.tile([P, PACK, P, 2], BF16, name="wc_late")
        woven = {u: ring.tile([P, P, PACK], BF16, name="woven", align_bytes=64) for u in range(EARLY)}
        for t in range(PACK):
            ga = keep.tile([P, R], F32, name="ga%d" % t)
            gb = keep.tile([P, R], F32, name="gb%d" % t)
            ga4 = ga[:].rearrange("p (m u) -> p m u", u=PACK)
            gb4 = gb[:].rearrange("p (m u) -> p m u", u=PACK)
            nc.scalar.activation(ga[:], ua_rows[t][:].indirect(l2[:]), ACT.Copy, scale=ha4[:, t : t + 1])
            for lo, hi in [(0, R)] if t < LAST else [(0, R // 2), (R // 2, R)]:
                nc.scalar.activation(
                    gb[:, lo:hi], ub_rows[t][:].indirect(part(l3, lo, hi)), ACT.Copy, scale=hb4[:, t : t + 1]
                )
                ms = slice(lo // PACK, hi // PACK)
                for u in range(EARLY):
                    nc.vector.tensor_tensor(woven[u][:, ms, t], ga4[:, ms, u], gb4[:, ms, u], ALU.add)
                nc.vector.tensor_tensor(wc_late[:, t, ms], ga4[:, ms, EARLY:], gb4[:, ms, EARLY:], ALU.add)

        def weave(u):
            full = ring.tile([P, P, PACK], BF16, name="woven", align_bytes=64)
            nc.vector.tensor_copy(full[:], wc_late[:, :, :, u - EARLY].rearrange("p t m -> p m t"))
            return full

        a_parts = []
        for u in range(PACK):
            wq_w = keep.tile([P, P], U32, name="wq_w%d" % u, align_bytes=64)
            wq_sc = keep.tile([P, P], U8, name="wq_sc%d" % u, align_bytes=64)
            nc.vector.quantize_mx(
                out=wq_w[:].bitcast(FP8X4), scales=wq_sc[:], in_=woven[u][:].rearrange("p m t -> p (m t)")
            )
            parts = []
            for lo, hi in [(0, J // 2), (J // 2, J)] if u == 0 else [(0, J)]:
                a_ps = psum.tile([P, hi - lo], F32, name="a_ps", bufs=4)
                nc.tensor.matmul_mx(
                    out=a_ps[:], lhsT=wq_w[:].bitcast(FP8X4), lhsT_scale=wq_sc[:],
                    rhs=xj_w[:, lo:hi].bitcast(FP8X4), rhs_scale=xj_sc[:, lo:hi], start=True, stop=True,
                )
                parts.append((lo, hi, a_ps))
            a_parts.append(parts)
            if u + 2 < PACK:
                woven[u + 2] = weave(u + 2)
            if u == 0:
                a_first = keep.tile([P, J], F32, name="a_sb0")
                for lo, hi, a_ps in parts:
                    nc.scalar.copy(a_first[:, lo:hi], a_ps[:])

        H = O // 2
        for u in range(PACK):
            if u == 0:
                a_sb = a_first
            else:
                a_sb = keep.tile([P, J], F32, name="a_sb%d" % u, tag="a_sb%d" % u)
                a_ps = a_parts[u][0][2]
                if u == 1:
                    nc.vector.tensor_copy(a_sb[:], a_ps[:])
                else:
                    nc.scalar.copy(a_sb[:], a_ps[:])
            h1 = keep.tile([P, S], F32, name="h1_%d" % u, tag="a_sb3" if u == 1 else "h1_%d" % u)
            nc.scalar.activation(h1[:], a_sb[:].indirect(l4[:]), ACT.Copy, scale=sa4[:, u : u + 1])
            if u == 0:
                pos = h1
            else:
                pos = keep.tile([P, S], F32, name="pos%d" % u, tag="pos%d" % u, align_bytes=64)
                nc.scalar.activation(pos[:], h1[:], ACT.Relu)
            nc.vector.tensor_copy(board[u][:].indirect(l5[:]), pos[:])

        xo_w = keep.tile([P, O], U32, name="xo_w", tag="pos3", align_bytes=64)
        nc.vector.tensor_copy(xo_w[:], xt_win[:].indirect(l7[:]))
        y_ps = {}
        for h in range(2):
            for nt in range(N // P):
                y_ps[h, nt] = psum.tile([P, H], F32, name="y_ps%d%d" % (h, nt))
                nc.tensor.matmul_mx(
                    out=y_ps[h, nt][:],
                    lhsT=ws_w[:, 2 * P * nt : 2 * P * (nt + 1)].bitcast(FP4X4),
                    lhsT_scale=ws_sc[:, P * nt : P * (nt + 1)],
                    rhs=xo_w[:, H * h : H * (h + 1)].bitcast(FP8X4),
                    rhs_scale=xo_sc[:, H * h : H * (h + 1)],
                    start=True, stop=False,
                )

        g1_first = keep.tile([P, C], F32, name="g1_first", tag="a_sb3")
        nc.scalar.activation(g1_first[:], board[0][:], ACT.Relu)
        g1 = [g1_first] + board[1:]

        hid = keep.tile([P, PACK, O], BF16, name="hid", tag="h1_3")
        for u in range(PACK):
            pieces = [(0, O)] if u < PACK - 1 else [(0, H), (H, O)]
            for lo, hi in pieces:
                nc.scalar.activation(
                    hid[:, u, lo:hi], g1[u][:].indirect(part(l6, lo, hi)), ACT.Copy, scale=sb4[:, u : u + 1]
                )

        for h in range(2):
            hw = keep.tile([P, H, PACK], BF16, name="hw%d" % h, align_bytes=64)
            nc.vector.tensor_copy(hw[:], hid[:, :, H * h : H * (h + 1)].rearrange("p t o -> p o t"))
            hq_w = keep.tile([P, H], U32, name="hq_w%d" % h, align_bytes=64)
            hq_sc = keep.tile([P, H], U8, name="hq_sc%d" % h, align_bytes=64)
            nc.vector.quantize_mx(
                out=hq_w[:].bitcast(FP8X4), scales=hq_sc[:], in_=hw[:].rearrange("p o t -> p (o t)")
            )
            res = keep.tile([P, N // P, H], F32, name="res%d" % h)
            for nt in range(N // P):
                nc.tensor.matmul_mx(
                    out=y_ps[h, nt][:],
                    lhsT=wb_w[:, P * nt : P * (nt + 1)].bitcast(FP8X4),
                    lhsT_scale=wb_sc[:, P * nt : P * (nt + 1)],
                    rhs=hq_w[:].bitcast(FP8X4), rhs_scale=hq_sc[:],
                    start=False, stop=True,
                )
                if nt == 0:
                    nc.scalar.copy(res[:, nt, :], y_ps[h, nt][:])
                else:
                    nc.vector.tensor_copy(res[:, nt, :], y_ps[h, nt][:])
            nc.sync.dma_start(out[:, H * h : H * (h + 1)].rearrange("(n p) o -> p n o", p=P), res[:])
